import numpy as np
import ml_dtypes


def mxq(x, axis, fmt="e4m3"):
    dtype, down = {"e4m3": (ml_dtypes.float8_e4m3fn, 7), "e5m2": (ml_dtypes.float8_e5m2, 14)}[fmt]
    v = np.moveaxis(np.asarray(x, np.float32).astype(ml_dtypes.bfloat16).astype(np.float64), axis, -1)
    blocks = v.reshape(v.shape[:-1] + (-1, 32))
    amax = np.abs(blocks).max(-1, keepdims=True)
    byte = np.maximum(np.where(amax > 0, np.frexp(amax)[1] - 1 + 127, 0) - down, 1)
    scale = np.exp2(byte - 127.0)
    codes = (blocks / scale).astype(np.float32).astype(dtype).astype(np.float64)
    return np.moveaxis((codes * scale).reshape(v.shape), -1, axis)


WIDE = False


def mx_kscale(k):
    if not WIDE:
        return np.ones(k)
    levels = np.array([10, -10, 5, -5, 0])
    if k % 512:
        return np.exp2(np.random.permutation(np.resize(levels, k // 32))).repeat(32)
    a = np.empty((k // 512, 16))
    for p in range(k // 512):
        a[p, :8] = np.random.permutation(np.resize(levels, 8))
        for g in range(8):
            far = levels[np.abs(levels - a[p, g]) >= 10]
            a[p, g + 8] = far[np.random.randint(len(far))]
    return np.exp2(a.ravel()).repeat(32)


def f64(x):
    return np.asarray(x).astype(np.float64)


def striped(idx):
    return np.tile(idx.reshape(-1, 16).T, (8, 1)).astype(np.uint16)


def unstriped(offs):
    return offs[:16].T.reshape(-1).astype(np.int64)


E2M1 = np.array([0.0, 0.5, 1.0, 1.5, 2.0, 3.0, 4.0, 6.0, -0.0, -0.5, -1.0, -1.5, -2.0, -3.0, -4.0, -6.0])


def pack_weight(w, fmt):
    k, n = w.shape
    w = f64(np.asarray(w, np.float32).astype(ml_dtypes.bfloat16)).reshape(k // 32, 32, n)
    amax = np.abs(w).max(1)
    if fmt == "e4m3":
        byte = np.frexp(amax)[1] - 1 + 127 - 7
    else:
        mant, ex = np.frexp(amax / 6.0)
        byte = np.where(mant > 0.5, ex, ex - 1) + 127
    byte = np.clip(np.where(amax > 0, byte, 1), 1, 254)
    scaled = (w * np.exp2(127.0 - byte)[:, None, :]).reshape(k, n).astype(np.float32)
    by_word = np.ascontiguousarray(scaled.reshape(k // 512, 128, 4, n).transpose(0, 1, 3, 2))
    if fmt == "e4m3":
        words = by_word.astype(ml_dtypes.float8_e4m3fn).view(np.uint8)
    else:
        c = by_word.astype(ml_dtypes.float4_e2m1fn).view(np.uint8) & 0xF
        words = (c[..., 0::2] | (c[..., 1::2] << 4)).reshape(k // 512, 128, 2 * n)
    return np.ascontiguousarray(words), np.ascontiguousarray(byte.astype(np.uint8).reshape(k // 512, 16, n))


def unpack_weight(words, scales, fmt):
    g, _, n = scales.shape
    words = np.ascontiguousarray(words).reshape(g, 128, n, -1)
    if fmt == "e4m3":
        vals = words.view(ml_dtypes.float8_e4m3fn).astype(np.float64)
    else:
        nib = np.empty((g, 128, n, 4), np.uint8)
        nib[..., 0::2] = words & 0xF
        nib[..., 1::2] = words >> 4
        vals = E2M1[nib]
    vals = vals * np.repeat(np.exp2(scales.astype(np.float64) - 127.0), 8, axis=1)[..., None]
    return vals.transpose(0, 1, 3, 2).reshape(g * 512, n)


def gelu(v):
    return 0.5 * v * (1.0 + np.tanh(np.sqrt(2.0 / np.pi) * (v + 0.044715 * v**3)))


K, T, S, T2, H, N = 1024, 2048, 512, 1024, 1536, 512

def setup_inputs():
    n = np.random.standard_normal
    s = mx_kscale(K)[:, None]
    u = mx_kscale(H)[:, None]
    tab_words, tab_scales = pack_weight(n((K, T)) * s, "e4m3")
    tab2_words, tab2_scales = pack_weight(n((K, T)) * s, "e4m3")
    w2_words, w2_scales = pack_weight(1.5 * n((K, H)) / np.sqrt(K) / s, "e2m1")
    perm = np.random.permutation(T2)
    return {
        "tab_words": tab_words, "tab_scales": tab_scales,
        "tab2_words": tab2_words, "tab2_scales": tab2_scales,
        "offs": striped(np.random.permutation(T)[:S]),
        "offs2": striped(np.random.permutation(T)[:S]),
        "offs3": striped(perm[:S]),
        "offs4": striped(perm[S:]),
        "w1": (1.5 * n((K, H)) / np.sqrt(K) / s).astype(np.float32),
        "w2_words": w2_words, "w2_scales": w2_scales,
        "wg1": np.exp(0.3 * n((128, S))).astype(np.float32),
        "wg2": np.exp(0.3 * n((128, S))).astype(np.float32),
        "xt": ((0.5 + n((H, T2))) * u).astype(np.float32),
        "w3": (n((H, N)) / np.sqrt(H) / u).astype(np.float32),
    }

def reference(tab_words, tab_scales, tab2_words, tab2_scales, offs, offs2, offs3, offs4,
              w1, w2_words, w2_scales, wg1, wg2, xt, w3):
    v = unpack_weight(tab_words, tab_scales, "e4m3")[:, unstriped(offs)]
    v2 = unpack_weight(tab2_words, tab2_scales, "e4m3")[:, unstriped(offs2)]
    a = mxq(f64(w1), 0, "e4m3").T @ v
    h1 = np.sqrt(1.0 + np.square(a))
    b = unpack_weight(w2_words, w2_scales, "e2m1").T @ v2
    h2 = np.abs(b)
    page = np.zeros((H, T2))
    page[:, unstriped(offs3)] = np.tile(f64(wg1), (H // 128, 1)) * h1
    page[:, unstriped(offs4)] = np.tile(f64(wg2), (H // 128, 1)) * h2
    z = np.maximum(page * f64(xt), 0.0)
    return mxq(f64(w3), 0, "e4m3").T @ mxq(z, 0, "e4m3")

@@ -1,0 +1,315 @@
+from contextlib import ExitStack
+
+import concourse.mybir as mybir
+
+K, T, S, T2, H, N = 1024, 2048, 512, 1024, 1536, 512
+FLOPS = 2 * (2 * K * H * S + H * N * T2)
+
+F32 = mybir.dt.float32
+BF16 = mybir.dt.bfloat16
+I32 = mybir.dt.int32
+U32 = mybir.dt.uint32
+U16 = mybir.dt.uint16
+U8 = mybir.dt.uint8
+E4M3 = mybir.dt.float8_e4m3fn_x4
+E2M1 = mybir.dt.float4_e2m1fn_x4
+ACT = mybir.ActivationFunctionType
+ALU = mybir.AluOpType
+
+P = 128
+PACK = 4
+PASS = P * PACK
+K_PASSES = K // PASS
+GROUPS = H // PASS
+QUADS = 4
+QUAD = P // QUADS
+BANK = 512
+BANKS = 8
+
+
+def tile_list_calorimeter_weave_kernel(
+    tc, tab_words, tab_scales, tab2_words, tab2_scales, offs, offs2, offs3, offs4,
+    w1, w2_words, w2_scales, wg1, wg2, xt, w3, out,
+):
+    nc = tc.nc
+    with ExitStack() as ctx:
+        keep = ctx.enter_context(tc.tile_pool(name="keep", bufs=1))
+        ring = ctx.enter_context(tc.tile_pool(name="ring", bufs=1))
+        psum = ctx.enter_context(tc.psum_pool(name="psum", bufs=1))
+
+        def load_list(src, name):
+            lst = keep.tile([P, S // 16], U16, name=name)
+            nc.sync.dma_start(lst[:], src)
+            return lst
+
+        def load_words(src, a, name):
+            words = keep.tile([P, T], I32, name=name, align_bytes=64)
+            nc.sync.dma_start(words[:], src[a].rearrange("p t i -> p (t i)").bitcast(I32))
+            return words
+
+        def gather(window, lst, dtype, name):
+            picked = keep.tile([P, S], dtype, name=name, align_bytes=64)
+            nc.vector.tensor_copy(picked[:], window.indirect(lst[:]))
+            return picked
+
+        def load_gain(src, name):
+            gain = keep.tile([P, PACK, S], F32, name=name)
+            for q in (0, 2, 1, 3):
+                nc.sync.dma_start(gain[QUAD * q : QUAD * (q + 1)], src.rearrange("(m t) j -> m t j", t=PACK))
+            return gain
+
+        def load_rows(src, name):
+            raw = ring.tile([P, PACK, BANK], F32, name=name, tag="raw", bufs=3)
+            nc.sync.dma_start(raw[:], src.rearrange("(p i) c -> p i c", i=PACK))
+            return raw
+
+        def load_xt(g):
+            fac = ring.tile([P, PACK, T2], F32, name=f"xt{g}", tag="xt", bufs=2)
+            rows = xt[PASS * g : PASS * (g + 1), :].rearrange("(p t) m -> p t m", t=PACK)
+            for half in range(2):
+                nc.sync.dma_start(fac[:, 2 * half : 2 * half + 2, :], rows[:, 2 * half : 2 * half + 2, :])
+            return fac
+
+        def bank(b, name):
+            return psum.tile([P, BANK], F32, name=name, tag=f"bank{b}")
+
+        tab2_s = keep.tile([P, K_PASSES, T], U8, name="tab2_s", align_bytes=64)
+        w2_s_raw = keep.tile([P, K_PASSES, H], U8, name="w2_s_raw", align_bytes=64)
+        tab_s = keep.tile([P, T], U8, name="tab_s", align_bytes=64)
+        nc.vector.memset(tab2_s[:].bitcast(I32), 0)
+        nc.vector.memset(w2_s_raw[:].bitcast(I32), 0)
+        nc.vector.memset(tab_s[:].bitcast(I32), 0)
+
+        tab2_w = [load_words(tab2_words, 0, "tab2_w0")]
+        list2 = load_list(offs2, "list2")
+        for q in range(QUADS):
+            nc.sync.dma_start(
+                tab2_s[QUAD * q : QUAD * q + 4].bitcast(I32),
+                tab2_scales[:, 4 * q : 4 * q + 4, :].rearrange("a r t -> r a t").bitcast(I32),
+            )
+        for q in range(QUADS):
+            nc.gpsimd.dma_start(
+                w2_s_raw[QUAD * q : QUAD * q + 4].bitcast(I32),
+                w2_scales[:, 4 * q : 4 * q + 4, :].rearrange("a r c -> r a c").bitcast(I32),
+            )
+        w2_w_raw = keep.tile([P, K_PASSES, H // 2], I32, name="w2_w_raw", align_bytes=64)
+        nc.sync.dma_start(w2_w_raw[:], w2_words.rearrange("a p c -> p a c").bitcast(I32))
+        tab2_w.append(load_words(tab2_words, 1, "tab2_w1"))
+        list4 = load_list(offs4, "list4")
+        gain2 = load_gain(wg2, "gain2")
+
+        def load_w1(g):
+            return [
+                load_rows(w1[PASS * a : PASS * (a + 1), PASS * g : PASS * (g + 1)], f"w1_raw{g}{a}")
+                for a in range(K_PASSES)
+            ]
+
+        w1_raw = load_w1(0)
+        list1 = load_list(offs, "list1")
+        for q in range(QUADS):
+            nc.sync.dma_start(
+                tab_s[QUAD * q : QUAD * q + 4 * K_PASSES].bitcast(I32),
+                tab_scales[:, 4 * q : 4 * q + 4, :].bitcast(I32),
+            )
+        tab_w = [load_words(tab_words, a, f"tab_w{a}") for a in range(K_PASSES)]
+        list3 = load_list(offs3, "list3")
+        gain1 = load_gain(wg1, "gain1")
+
+        v2_w = [gather(tab2_w[0][:].bitcast(U32), list2, U32, "v2_w0")]
+        v2_s = [gather(tab2_s[:, a, :], list2, U8, f"v2_s{a}") for a in range(K_PASSES)]
+
+        def order_w2(groups, name):
+            n = len(groups)
+            cols = slice(PASS * groups[0], PASS * (groups[-1] + 1))
+            words = keep.tile([P, K_PASSES, n * PASS], U16, name=name + "_w", align_bytes=64)
+            scales = keep.tile([P, K_PASSES, n * PASS], U8, name=name + "_s", align_bytes=64)
+            nc.vector.tensor_copy(
+                words[:].rearrange("p a (g t m) -> p a g t m", g=n, t=PACK),
+                w2_w_raw[:].bitcast(U16)[:, :, cols].rearrange("p a (g m t) -> p a g t m", g=n, t=PACK),
+            )
+            nc.vector.tensor_copy(
+                scales[:].rearrange("p a (g t m) -> p a g t m", g=n, t=PACK),
+                w2_s_raw[:, :, cols].rearrange("p a (g m t) -> p a g t m", g=n, t=PACK),
+            )
+            return {g: (words, scales, PASS * i) for i, g in enumerate(groups)}
+
+        w2_q = order_w2([0], "w2_first")
+        v2_w.append(gather(tab2_w[1][:].bitcast(U32), list2, U32, "v2_w1"))
+        w2_q = {**w2_q, **order_w2(list(range(1, GROUPS)), "w2_rest")}
+
+        uses = [0]
+
+        def next_bank(name):
+            uses[0] = uses[0] + 1
+            return bank(uses[0] % BANKS, name)
+
+        def response2(g, t):
+            words, scales, col0 = w2_q[g]
+            cols = slice(col0 + P * t, col0 + P * (t + 1))
+            acc = next_bank(f"b{g}{t}")
+            for a in range(K_PASSES):
+                nc.tensor.matmul_mx(
+                    out=acc[:],
+                    lhsT=words[:, a, cols].bitcast(E2M1), lhsT_scale=scales[:, a, cols],
+                    rhs=v2_w[a][:].bitcast(E4M3), rhs_scale=v2_s[a][:],
+                    start=(a == 0), stop=(a == K_PASSES - 1),
+                )
+            h = ring.tile([P, S], F32, name=f"h2_{g}{t}", tag="h", bufs=8)
+            nc.scalar.activation(h[:], acc[:], ACT.Abs)
+            return h
+
+        def round_w1(raws, g):
+            rounded = ring.tile([P, K_PASSES, PASS * PACK], BF16, name=f"w1_bf{g}", tag="bf", bufs=2, align_bytes=64)
+            for a in range(K_PASSES):
+                nc.scalar.copy(
+                    rounded[:, a, :].rearrange("p (t m i) -> p m i t", t=PACK, i=PACK),
+                    raws[a][:].rearrange("p i (m t) -> p m i t", t=PACK),
+                )
+            return rounded
+
+        def quantize(rounded, width, name, tag, bufs):
+            codes = ring.tile([P, width], U32, name=name + "_w", tag=tag + "_w", bufs=bufs, align_bytes=64)
+            scales = ring.tile([P, width], U8, name=name + "_s", tag=tag + "_s", bufs=bufs, align_bytes=64)
+            nc.vector.quantize_mx(out=codes[:].bitcast(E4M3), scales=scales[:], in_=rounded)
+            return codes, scales
+
+        def quantize_w1(rounded, g):
+            return quantize(rounded[:].rearrange("p a c -> p (a c)"), K_PASSES * PASS, f"w1_q{g}", "w1_q", 2)
+
+        def response1(g, t):
+            codes, scales = w1_q[g]
+            acc = next_bank(f"a{g}{t}")
+            for a in range(K_PASSES):
+                cols = slice(PASS * a + P * t, PASS * a + P * (t + 1))
+                nc.tensor.matmul_mx(
+                    out=acc[:],
+                    lhsT=codes[:, cols].bitcast(E4M3), lhsT_scale=scales[:, cols],
+                    rhs=v_w[a][:].bitcast(E4M3), rhs_scale=v_s[4 * a : P, :],
+                    start=(a == 0), stop=(a == K_PASSES - 1),
+                )
+            h = ring.tile([P, S], F32, name=f"h1_{g}{t}", tag="h", bufs=8)
+            nc.scalar.activation(h[:], acc[:], ACT.Square)
+            nc.scalar.activation(h[:], h[:], ACT.Sqrt, bias=1.0)
+            return h
+
+        pages = {}
+
+        def scatter2(g, t):
+            pages[g, t] = ring.tile([P, T2], F32, name=f"page{g}{t}", tag="page", bufs=7)
+            nc.vector.tensor_tensor(pages[g, t][:].indirect(list4[:]), h2[g, t][:], gain2[:, t, :], ALU.mult)
+
+        def scatter1(g, t):
+            nc.vector.tensor_tensor(pages[g, t][:].indirect(list3[:]), h1[g, t][:], gain1[:, t, :], ALU.mult)
+
+        def crosstalk(g, t, cols):
+            nc.vector.tensor_tensor(fac[g][:, t, cols], pages[g, t][:, cols], fac[g][:, t, cols], ALU.mult)
+
+        def weave_views(dst, src):
+            return (
+                dst.rearrange("p (c i t) -> p c t i", t=PACK, i=4),
+                src.rearrange("p t (c i) -> p c t i", i=4),
+            )
+
+        def round_w3(raw, g):
+            rounded = ring.tile([P, N * PACK], BF16, name=f"w3_bf{g}", tag="bf", bufs=2, align_bytes=64)
+            nc.scalar.copy(*weave_views(rounded[:], raw[:]))
+            return rounded
+
+        def round_z(g):
+            rounded = ring.tile([P, T2 * PACK], BF16, name=f"z_bf{g}", tag="bf", bufs=2, align_bytes=64)
+            dst, src = weave_views(rounded[:], fac[g][:])
+            nc.scalar.activation(dst, src, ACT.Relu)
+            return rounded
+
+        h1, h2, fac, w1_q, w3_q, z_q = {}, {}, {}, {}, {}, {}
+        everything = slice(0, T2)
+
+        for t in range(PACK):
+            h2[0, t] = response2(0, t)
+        w1_bf = round_w1(w1_raw, 0)
+        fac[0] = load_xt(0)
+        scatter2(0, 0)
+        scatter2(0, 1)
+        w1_q[0] = quantize_w1(w1_bf, 0)
+        v_s = gather(tab_s[:], list1, U8, "v_s")
+        v_w = [gather(tab_w[a][:].bitcast(U32), list1, U32, f"v_w{a}") for a in range(K_PASSES)]
+        for t in range(2):
+            h1[0, t] = response1(0, t)
+            h2[1, t] = response2(1, t)
+        scatter2(0, 2)
+        scatter2(0, 3)
+
+        last = GROUPS - 1
+        for g in range(last):
+            w1_raw = load_w1(g + 1)
+            w3_raw = load_rows(w3[PASS * g : PASS * (g + 1), :], f"w3_raw{g}")
+            fac[g + 1] = load_xt(g + 1)
+            for t in range(PACK):
+                if t == 0:
+                    w1_bf = round_w1(w1_raw, g + 1)
+                if t == 1:
+                    w1_q[g + 1] = quantize_w1(w1_bf, g + 1)
+                    w3_bf = round_w3(w3_raw, g)
+                if t == 2:
+                    w3_q[g] = quantize(w3_bf[:], N, f"w3_q{g}", "w3_q", GROUPS)
+                ahead_g, ahead_t = divmod(PACK * g + t + 2, PACK)
+                h1[ahead_g, ahead_t] = response1(ahead_g, ahead_t)
+                if ahead_g < last:
+                    h2[ahead_g + 1, ahead_t] = response2(ahead_g + 1, ahead_t)
+                scatter1(g, t)
+                scatter2(g + 1, t)
+                crosstalk(g, t, everything)
+                if t == 0 and g > 0:
+                    z_q[g - 1] = quantize(z_bf[:], T2, f"z_q{g - 1}", "z_q", GROUPS)
+            z_bf = round_z(g)
+
+        w3_raw = load_rows(w3[PASS * last : PASS * (last + 1), :], f"w3_raw{last}")
+        for t in range(2, PACK):
+            h1[last, t] = response1(last, t)
+        w3_bf = round_w3(w3_raw, last)
+        scatter1(last, 0)
+        z_q[last - 1] = quantize(z_bf[:], T2, f"z_q{last - 1}", "z_q", GROUPS)
+        w3_q[last] = quantize(w3_bf[:], N, f"w3_q{last}", "w3_q", GROUPS)
+
+        sums = {(half, n): bank(4 * half + n, f"sum{half}{n}") for half in range(2) for n in range(N // P)}
+
+        def product(g, half, z_codes, z_scales, cols):
+            codes, scales = w3_q[g]
+            for n in range(N // P):
+                rows = slice(P * n, P * (n + 1))
+                nc.tensor.matmul_mx(
+                    out=sums[half, n][:],
+                    lhsT=codes[:, rows].bitcast(E4M3), lhsT_scale=scales[:, rows],
+                    rhs=z_codes[:, cols].bitcast(E4M3), rhs_scale=z_scales[:, cols],
+                    start=(g == 0), stop=(g == last),
+                )
+
+        for g in range(last):
+            for half in range(2):
+                product(g, half, *z_q[g], slice(BANK * half, BANK * (half + 1)))
+        for t in range(1, PACK):
+            scatter1(last, t)
+            crosstalk(last, t - 1, everything)
+
+        halves = [slice(BANK * half, BANK * (half + 1)) for half in range(2)]
+        for cols in halves:
+            crosstalk(last, PACK - 1, cols)
+        z_last = [
+            ring.tile([P, BANK * PACK], BF16, name=f"z_last{half}", tag="bf", bufs=2, align_bytes=64)
+            for half in range(2)
+        ]
+        dst, src = weave_views(z_last[0][:], fac[last][:, :, halves[0]])
+        nc.vector.tensor_scalar_max(dst, src, 0.0)
+        dst, src = weave_views(z_last[1][:], fac[last][:, :, halves[1]])
+        nc.scalar.activation(dst, src, ACT.Relu)
+        for half in range(2):
+            codes, scales = quantize(z_last[half][:], BANK, f"z_last_q{half}", "z_last_q", 2)
+            product(last, half, codes, scales, slice(0, BANK))
+        for half in range(2):
+            result = ring.tile([P, N // P, BANK], F32, name=f"result{half}", tag="raw", bufs=3)
+            for n in range(N // P):
+                if n % 2 == 0:
+                    nc.vector.tensor_copy(result[:, n, :], sums[half, n][:])
+                else:
+                    nc.scalar.copy(result[:, n, :], sums[half, n][:])
+                nc.sync.dma_start(out[P * n : P * (n + 1), halves[half]], result[:, n, :])

@@ -1,6 +1,7 @@
 from contextlib import ExitStack
 
 import concourse.mybir as mybir
+from concourse.masks import make_identity
 
 K, T, S, T2, H, N = 1024, 2048, 512, 1024, 1536, 512
 FLOPS = 2 * (2 * K * H * S + H * N * T2)
@@ -25,6 +26,9 @@ QUADS = 4
 QUAD = P // QUADS
 BANK = 512
 BANKS = 8
+RUN = 4
+RUNS = P // RUN
+CHUNK = 256
 
 
 def tile_list_calorimeter_weave_kernel(
@@ -53,10 +57,13 @@ def tile_list_calorimeter_weave_kernel(
             return picked
 
         def load_gain(src, name):
-            gain = keep.tile([P, PACK, S], F32, name=name)
-            for q in (0, 2, 1, 3):
-                nc.sync.dma_start(gain[QUAD * q : QUAD * (q + 1)], src.rearrange("(m t) j -> m t j", t=PACK))
-            return gain
+            raw = keep.tile([P, S], F32, name=name)
+            nc.sync.dma_start(raw[:], src)
+            return raw
+
+        def load_by_slot(tile, rows):
+            for t in range(PACK):
+                nc.sync.dma_start(tile[:, t, :], rows.rearrange("(e t u) c -> t e u c", t=PACK, u=RUN)[t])
 
         def load_rows(src, name):
             raw = ring.tile([P, PACK, BANK], F32, name=name, tag="raw", bufs=3)
@@ -65,9 +72,7 @@ def tile_list_calorimeter_weave_kernel(
 
         def load_xt(g):
             fac = ring.tile([P, PACK, T2], F32, name=f"xt{g}", tag="xt", bufs=2)
-            rows = xt[PASS * g : PASS * (g + 1), :].rearrange("(p t) m -> p t m", t=PACK)
-            for half in range(2):
-                nc.sync.dma_start(fac[:, 2 * half : 2 * half + 2, :], rows[:, 2 * half : 2 * half + 2, :])
+            load_by_slot(fac, xt[PASS * g : PASS * (g + 1), :])
             return fac
 
         def bank(b, name):
@@ -76,27 +81,28 @@ def tile_list_calorimeter_weave_kernel(
         tab2_s = keep.tile([P, K_PASSES, T], U8, name="tab2_s", align_bytes=64)
         w2_s_raw = keep.tile([P, K_PASSES, H], U8, name="w2_s_raw", align_bytes=64)
         tab_s = keep.tile([P, T], U8, name="tab_s", align_bytes=64)
-        nc.vector.memset(tab2_s[:].bitcast(I32), 0)
+        nc.gpsimd.memset(tab2_s[:].bitcast(I32), 0)
         nc.vector.memset(w2_s_raw[:].bitcast(I32), 0)
         nc.vector.memset(tab_s[:].bitcast(I32), 0)
 
-        tab2_w = [load_words(tab2_words, 0, "tab2_w0")]
         list2 = load_list(offs2, "list2")
+        wg2_raw = load_gain(wg2, "wg2_raw")
+        tab2_w = [load_words(tab2_words, 0, "tab2_w0")]
         for q in range(QUADS):
             nc.sync.dma_start(
                 tab2_s[QUAD * q : QUAD * q + 4].bitcast(I32),
                 tab2_scales[:, 4 * q : 4 * q + 4, :].rearrange("a r t -> r a t").bitcast(I32),
             )
+        w2_w_raw = ring.tile([P, K_PASSES, H // 2], I32, name="w2_w_raw", tag="raw", bufs=3)
+        nc.sync.dma_start(w2_w_raw[:], w2_words.rearrange("a p c -> p a c").bitcast(I32))
+        tab2_w.append(load_words(tab2_words, 1, "tab2_w1"))
         for q in range(QUADS):
-            nc.gpsimd.dma_start(
+            nc.sync.dma_start(
                 w2_s_raw[QUAD * q : QUAD * q + 4].bitcast(I32),
                 w2_scales[:, 4 * q : 4 * q + 4, :].rearrange("a r c -> r a c").bitcast(I32),
             )
-        w2_w_raw = keep.tile([P, K_PASSES, H // 2], I32, name="w2_w_raw", align_bytes=64)
-        nc.sync.dma_start(w2_w_raw[:], w2_words.rearrange("a p c -> p a c").bitcast(I32))
-        tab2_w.append(load_words(tab2_words, 1, "tab2_w1"))
+
         list4 = load_list(offs4, "list4")
-        gain2 = load_gain(wg2, "gain2")
 
         def load_w1(g):
             return [
@@ -104,7 +110,6 @@ def tile_list_calorimeter_weave_kernel(
                 for a in range(K_PASSES)
             ]
 
-        w1_raw = load_w1(0)
         list1 = load_list(offs, "list1")
         for q in range(QUADS):
             nc.sync.dma_start(
@@ -112,30 +117,24 @@ def tile_list_calorimeter_weave_kernel(
                 tab_scales[:, 4 * q : 4 * q + 4, :].bitcast(I32),
             )
         tab_w = [load_words(tab_words, a, f"tab_w{a}") for a in range(K_PASSES)]
+        wg1_raw = load_gain(wg1, "wg1_raw")
+        w1_raw = {0: load_w1(0)}
         list3 = load_list(offs3, "list3")
-        gain1 = load_gain(wg1, "gain1")
 
         v2_w = [gather(tab2_w[0][:].bitcast(U32), list2, U32, "v2_w0")]
         v2_s = [gather(tab2_s[:, a, :], list2, U8, f"v2_s{a}") for a in range(K_PASSES)]
 
-        def order_w2(groups, name):
-            n = len(groups)
-            cols = slice(PASS * groups[0], PASS * (groups[-1] + 1))
-            words = keep.tile([P, K_PASSES, n * PASS], U16, name=name + "_w", align_bytes=64)
-            scales = keep.tile([P, K_PASSES, n * PASS], U8, name=name + "_s", align_bytes=64)
-            nc.vector.tensor_copy(
-                words[:].rearrange("p a (g t m) -> p a g t m", g=n, t=PACK),
-                w2_w_raw[:].bitcast(U16)[:, :, cols].rearrange("p a (g m t) -> p a g t m", g=n, t=PACK),
-            )
-            nc.vector.tensor_copy(
-                scales[:].rearrange("p a (g t m) -> p a g t m", g=n, t=PACK),
-                w2_s_raw[:, :, cols].rearrange("p a (g m t) -> p a g t m", g=n, t=PACK),
-            )
-            return {g: (words, scales, PASS * i) for i, g in enumerate(groups)}
-
-        w2_q = order_w2([0], "w2_first")
+        w2_w = keep.tile([P, K_PASSES * H // 2], I32, name="w2_w", align_bytes=64)
+        w2_s = keep.tile([P, K_PASSES * H // 4], I32, name="w2_s", align_bytes=64)
+        nc.vector.tensor_copy(
+            w2_w[:].rearrange("p (b t e w) -> p b t e w", t=PACK, e=RUNS, w=2),
+            w2_w_raw[:].rearrange("p a (g e t w) -> p (a g) t e w", t=PACK, e=RUNS, w=2),
+        )
         v2_w.append(gather(tab2_w[1][:].bitcast(U32), list2, U32, "v2_w1"))
-        w2_q = {**w2_q, **order_w2(list(range(1, GROUPS)), "w2_rest")}
+        nc.vector.tensor_copy(
+            w2_s[:].rearrange("p (b t e) -> p b e t", t=PACK, e=RUNS),
+            w2_s_raw[:].bitcast(I32).rearrange("p a (g e t) -> p (a g) e t", t=PACK, e=RUNS),
+        )
 
         uses = [0]
 
@@ -143,29 +142,59 @@ def tile_list_calorimeter_weave_kernel(
             uses[0] = uses[0] + 1
             return bank(uses[0] % BANKS, name)
 
-        def response2(g, t):
-            words, scales, col0 = w2_q[g]
-            cols = slice(col0 + P * t, col0 + P * (t + 1))
-            acc = next_bank(f"b{g}{t}")
+        identity = keep.tile([P, P], F32, name="identity")
+        make_identity(nc, identity[:])
+
+        def order_gain(raw, name):
+            turned = next_bank(name + "_turned")
+            for c in range(S // P):
+                nc.tensor.transpose(turned[:, P * c : P * (c + 1)], raw[:, P * c : P * (c + 1)], identity[:])
+            spread = []
+            for c in range(S // P):
+                piece = ring.tile([P, PACK * P], F32, name=f"{name}_spread{c}", tag="h", bufs=6, align_bytes=64)
+                rows = turned[:, P * c : P * (c + 1)].rearrange("j (e t u) -> j t e u", t=PACK, u=RUN)
+                nc.scalar.copy(
+                    piece[:].rearrange("j (t q e u) -> j t q e u", t=PACK, q=QUADS, u=RUN),
+                    rows.unsqueeze(2).broadcast_to([P, PACK, QUADS, QUAD // RUN, RUN]),
+                )
+                spread.append(piece)
+            gain = keep.tile([P, PACK, S], F32, name=name)
+            for t in range(PACK):
+                back = next_bank(f"{name}_back{t}")
+                for c in range(S // P):
+                    nc.tensor.transpose(back[:, P * c : P * (c + 1)], spread[c][:, P * t : P * (t + 1)], identity[:])
+                nc.scalar.copy(gain[:, t, :], back[:])
+            return gain
+
+        gain2 = order_gain(wg2_raw, "gain2")
+
+        def response_tile(stream, page):
+            h = ring.tile([P, S], F32, name=f"h{stream}_{page}", tag="h", bufs=6, align_bytes=64)
+            return h[:]
+
+        def response2(page):
+            t = page % PACK
+            acc = next_bank(f"b{page}")
             for a in range(K_PASSES):
+                cols = slice(H * a + P * page, H * a + P * (page + 1))
                 nc.tensor.matmul_mx(
                     out=acc[:],
-                    lhsT=words[:, a, cols].bitcast(E2M1), lhsT_scale=scales[:, a, cols],
+                    lhsT=w2_w[:].bitcast(U16)[:, cols].bitcast(E2M1), lhsT_scale=w2_s[:].bitcast(U8)[:, cols],
                     rhs=v2_w[a][:].bitcast(E4M3), rhs_scale=v2_s[a][:],
                     start=(a == 0), stop=(a == K_PASSES - 1),
                 )
-            h = ring.tile([P, S], F32, name=f"h2_{g}{t}", tag="h", bufs=8)
-            nc.scalar.activation(h[:], acc[:], ACT.Abs)
-            return h
+            h = response_tile(2, page)
+            nc.scalar.activation(h, acc[:], ACT.Abs)
 
-        def round_w1(raws, g):
-            rounded = ring.tile([P, K_PASSES, PASS * PACK], BF16, name=f"w1_bf{g}", tag="bf", bufs=2, align_bytes=64)
+            resp[2, page] = h
+
+        def round_w1(g):
             for a in range(K_PASSES):
+                w1_bf[g, a] = ring.tile([P, PASS * PACK], BF16, name=f"w1_bf{g}{a}", tag=f"w1_bf{g}{a}", align_bytes=64)
                 nc.scalar.copy(
-                    rounded[:, a, :].rearrange("p (t m i) -> p m i t", t=PACK, i=PACK),
-                    raws[a][:].rearrange("p i (m t) -> p m i t", t=PACK),
+                    w1_bf[g, a][:].rearrange("p (t e u i) -> p e t i u", t=PACK, u=RUN, i=PACK),
+                    w1_raw[g][a][:].rearrange("p i (e t u) -> p e t i u", t=PACK, u=RUN),
                 )
-            return rounded
 
         def quantize(rounded, width, name, tag, bufs):
             codes = ring.tile([P, width], U32, name=name + "_w", tag=tag + "_w", bufs=bufs, align_bytes=64)
@@ -173,36 +202,41 @@ def tile_list_calorimeter_weave_kernel(
             nc.vector.quantize_mx(out=codes[:].bitcast(E4M3), scales=scales[:], in_=rounded)
             return codes, scales
 
-        def quantize_w1(rounded, g):
-            return quantize(rounded[:].rearrange("p a c -> p (a c)"), K_PASSES * PASS, f"w1_q{g}", "w1_q", 2)
-
-        def response1(g, t):
-            codes, scales = w1_q[g]
-            acc = next_bank(f"a{g}{t}")
+        def quantize_w1(g):
             for a in range(K_PASSES):
-                cols = slice(PASS * a + P * t, PASS * a + P * (t + 1))
+                w1_q[g, a] = quantize(w1_bf[g, a][:], PASS, f"w1_q{g}{a}", "w1_q", 2 * K_PASSES)
+
+        def response1(page):
+            g, t = divmod(page, PACK)
+            cols = slice(P * t, P * (t + 1))
+            acc = next_bank(f"a{page}")
+            for a in range(K_PASSES):
+                codes, scales = w1_q[g, a]
                 nc.tensor.matmul_mx(
                     out=acc[:],
                     lhsT=codes[:, cols].bitcast(E4M3), lhsT_scale=scales[:, cols],
                     rhs=v_w[a][:].bitcast(E4M3), rhs_scale=v_s[4 * a : P, :],
                     start=(a == 0), stop=(a == K_PASSES - 1),
                 )
-            h = ring.tile([P, S], F32, name=f"h1_{g}{t}", tag="h", bufs=8)
-            nc.scalar.activation(h[:], acc[:], ACT.Square)
-            nc.scalar.activation(h[:], h[:], ACT.Sqrt, bias=1.0)
-            return h
+            h = response_tile(1, page)
+            nc.scalar.activation(h, acc[:], ACT.Square)
+            nc.scalar.activation(h, h, ACT.Sqrt, bias=1.0)
 
-        pages = {}
+            resp[1, page] = h
 
-        def scatter2(g, t):
-            pages[g, t] = ring.tile([P, T2], F32, name=f"page{g}{t}", tag="page", bufs=7)
-            nc.vector.tensor_tensor(pages[g, t][:].indirect(list4[:]), h2[g, t][:], gain2[:, t, :], ALU.mult)
+        def scatter2(page):
+            if page in reuse:
+                pages[page] = ring.tile([P, T2], F32, name=f"page{page}", tag=reuse[page], align_bytes=64)
+            else:
+                pages[page] = ring.tile([P, T2], F32, name=f"page{page}", tag="page", bufs=4)
+            nc.vector.tensor_tensor(pages[page][:].indirect(list4[:]), resp[2, page], gain2[:, page % PACK, :], ALU.mult)
 
-        def scatter1(g, t):
-            nc.vector.tensor_tensor(pages[g, t][:].indirect(list3[:]), h1[g, t][:], gain1[:, t, :], ALU.mult)
+        def scatter1(page):
+            nc.vector.tensor_tensor(pages[page][:].indirect(list3[:]), resp[1, page], gain1[:, page % PACK, :], ALU.mult)
 
-        def crosstalk(g, t, cols):
-            nc.vector.tensor_tensor(fac[g][:, t, cols], pages[g, t][:, cols], fac[g][:, t, cols], ALU.mult)
+        def crosstalk(engine, page, cols):
+            g, t = divmod(page, PACK)
+            engine.tensor_tensor(fac[g][:, t, cols], pages[page][:, cols], fac[g][:, t, cols], ALU.mult)
 
         def weave_views(dst, src):
             return (
@@ -210,106 +244,130 @@ def tile_list_calorimeter_weave_kernel(
                 src.rearrange("p t (c i) -> p c t i", i=4),
             )
 
-        def round_w3(raw, g):
-            rounded = ring.tile([P, N * PACK], BF16, name=f"w3_bf{g}", tag="bf", bufs=2, align_bytes=64)
-            nc.scalar.copy(*weave_views(rounded[:], raw[:]))
-            return rounded
+        def round_w3(g):
+            raw = ring.tile([P, PACK, BANK], F32, name=f"w3_raw{g}", tag="raw", bufs=3)
+            load_by_slot(raw, w3[PASS * g : PASS * (g + 1), :])
+            w3_bf[g] = ring.tile([P, N * PACK], BF16, name=f"w3_bf{g}", tag="bf", bufs=2, align_bytes=64)
+            nc.scalar.copy(*weave_views(w3_bf[g][:], raw[:]))
 
         def round_z(g):
-            rounded = ring.tile([P, T2 * PACK], BF16, name=f"z_bf{g}", tag="bf", bufs=2, align_bytes=64)
-            dst, src = weave_views(rounded[:], fac[g][:])
-            nc.scalar.activation(dst, src, ACT.Relu)
-            return rounded
+            z_bf[g] = ring.tile([P, T2 * PACK], BF16, name=f"z_bf{g}", tag="bf", bufs=2, align_bytes=64)
+            for half in range(2):
+                dst, src = weave_views(
+                    z_bf[g][:, BANK * PACK * half : BANK * PACK * (half + 1)], fac[g][:, :, halves[half]]
+                )
+                nc.scalar.activation(dst, src, ACT.Relu)
 
-        h1, h2, fac, w1_q, w3_q, z_q = {}, {}, {}, {}, {}, {}
-        everything = slice(0, T2)
+        resp, pages, fac, w1_bf, w1_q, w3_bf, w3_q, z_bf, z_q = {}, {}, {}, {}, {}, {}, {}, {}, {}
+        halves = [slice(BANK * half, BANK * (half + 1)) for half in range(2)]
+        reuse = {3: "w1_bf00", 4: "w1_bf01", 7: "w1_bf10", 8: "w1_bf11", 10: "w1_bf20", 11: "w1_bf21"}
+        last = GROUPS - 1
+        n_pages = GROUPS * PACK
+        lead = 5
 
-        for t in range(PACK):
-            h2[0, t] = response2(0, t)
-        w1_bf = round_w1(w1_raw, 0)
+        for page in range(3):
+            response2(page)
+        gain1 = order_gain(wg1_raw, "gain1")
+        round_w1(0)
         fac[0] = load_xt(0)
-        scatter2(0, 0)
-        scatter2(0, 1)
-        w1_q[0] = quantize_w1(w1_bf, 0)
+        w1_raw[1] = load_w1(1)
+        for page in range(3):
+            scatter2(page)
         v_s = gather(tab_s[:], list1, U8, "v_s")
         v_w = [gather(tab_w[a][:].bitcast(U32), list1, U32, f"v_w{a}") for a in range(K_PASSES)]
-        for t in range(2):
-            h1[0, t] = response1(0, t)
-            h2[1, t] = response2(1, t)
-        scatter2(0, 2)
-        scatter2(0, 3)
+        quantize_w1(0)
+        response2(3)
+        response2(4)
+        response1(0)
+        response2(5)
+        response1(1)
+        scatter2(3)
+        scatter2(4)
+        round_w1(1)
+        fac[1] = load_xt(1)
+        w1_raw[2] = load_w1(2)
 
-        last = GROUPS - 1
-        for g in range(last):
-            w1_raw = load_w1(g + 1)
-            w3_raw = load_rows(w3[PASS * g : PASS * (g + 1), :], f"w3_raw{g}")
-            fac[g + 1] = load_xt(g + 1)
-            for t in range(PACK):
-                if t == 0:
-                    w1_bf = round_w1(w1_raw, g + 1)
-                if t == 1:
-                    w1_q[g + 1] = quantize_w1(w1_bf, g + 1)
-                    w3_bf = round_w3(w3_raw, g)
-                if t == 2:
-                    w3_q[g] = quantize(w3_bf[:], N, f"w3_q{g}", "w3_q", GROUPS)
-                ahead_g, ahead_t = divmod(PACK * g + t + 2, PACK)
-                h1[ahead_g, ahead_t] = response1(ahead_g, ahead_t)
-                if ahead_g < last:
-                    h2[ahead_g + 1, ahead_t] = response2(ahead_g + 1, ahead_t)
-                scatter1(g, t)
-                scatter2(g + 1, t)
-                crosstalk(g, t, everything)
-                if t == 0 and g > 0:
-                    z_q[g - 1] = quantize(z_bf[:], T2, f"z_q{g - 1}", "z_q", GROUPS)
-            z_bf = round_z(g)
+        for page in range(n_pages - 1):
+            if page == 1:
+                quantize_w1(1)
+            if page == 2:
+                round_w1(2)
+            if page == 4:
+                quantize_w1(2)
+            if page + 2 < n_pages:
+                if page + 1 + lead < n_pages:
+                    response2(page + 1 + lead)
+                response1(page + 2)
+            scatter1(page)
+            if page + lead < n_pages:
+                scatter2(page + lead)
+            crosstalk(nc.vector, page, slice(0, T2))
+            if page % PACK == PACK - 1:
+                round_z(page // PACK)
+                if page // PACK + 2 < GROUPS:
+                    fac[page // PACK + 2] = load_xt(page // PACK + 2)
+            if page % PACK == 1 and page > PACK:
+                g = page // PACK - 1
+                z_q[g] = quantize(z_bf[g][:], T2, f"z_q{g}", "z_q", last)
+            if page in (5, 6, 7):
+                round_w3(page - 5)
+            if page in (6, 7, 8):
+                w3_q[page - 6] = quantize(w3_bf[page - 6][:], N, f"w3_q{page - 6}", "w3_q", GROUPS)
 
-        w3_raw = load_rows(w3[PASS * last : PASS * (last + 1), :], f"w3_raw{last}")
-        for t in range(2, PACK):
-            h1[last, t] = response1(last, t)
-        w3_bf = round_w3(w3_raw, last)
-        scatter1(last, 0)
-        z_q[last - 1] = quantize(z_bf[:], T2, f"z_q{last - 1}", "z_q", GROUPS)
-        w3_q[last] = quantize(w3_bf[:], N, f"w3_q{last}", "w3_q", GROUPS)
+        chunks = [slice(CHUNK * c, CHUNK * (c + 1)) for c in range(T2 // CHUNK)]
+        sums = {(c, pair): bank(2 * c + pair, f"sum{c}{pair}") for c in range(len(chunks)) for pair in range(2)}
 
-        sums = {(half, n): bank(4 * half + n, f"sum{half}{n}") for half in range(2) for n in range(N // P)}
-
-        def product(g, half, z_codes, z_scales, cols):
+        def product(g, c, z_codes, z_scales, cols):
             codes, scales = w3_q[g]
             for n in range(N // P):
                 rows = slice(P * n, P * (n + 1))
+                pair, side = divmod(n, 2)
                 nc.tensor.matmul_mx(
-                    out=sums[half, n][:],
+                    out=sums[c, pair][:, CHUNK * side : CHUNK * (side + 1)],
                     lhsT=codes[:, rows].bitcast(E4M3), lhsT_scale=scales[:, rows],
                     rhs=z_codes[:, cols].bitcast(E4M3), rhs_scale=z_scales[:, cols],
-                    start=(g == 0), stop=(g == last),
+                    start=(g == 0 and side == 0), stop=(g == last and side == 1),
                 )
 
         for g in range(last):
-            for half in range(2):
-                product(g, half, *z_q[g], slice(BANK * half, BANK * (half + 1)))
-        for t in range(1, PACK):
-            scatter1(last, t)
-            crosstalk(last, t - 1, everything)
+            for c, cols in enumerate(chunks):
+                product(g, c, *z_q[g], cols)
+        scatter1(n_pages - 1)
 
-        halves = [slice(BANK * half, BANK * (half + 1)) for half in range(2)]
-        for cols in halves:
-            crosstalk(last, PACK - 1, cols)
-        z_last = [
-            ring.tile([P, BANK * PACK], BF16, name=f"z_last{half}", tag="bf", bufs=2, align_bytes=64)
-            for half in range(2)
-        ]
-        dst, src = weave_views(z_last[0][:], fac[last][:, :, halves[0]])
-        nc.vector.tensor_scalar_max(dst, src, 0.0)
-        dst, src = weave_views(z_last[1][:], fac[last][:, :, halves[1]])
-        nc.scalar.activation(dst, src, ACT.Relu)
-        for half in range(2):
-            codes, scales = quantize(z_last[half][:], BANK, f"z_last_q{half}", "z_last_q", 2)
-            product(last, half, codes, scales, slice(0, BANK))
-        for half in range(2):
-            result = ring.tile([P, N // P, BANK], F32, name=f"result{half}", tag="raw", bufs=3)
-            for n in range(N // P):
-                if n % 2 == 0:
-                    nc.vector.tensor_copy(result[:, n, :], sums[half, n][:])
+        z_last = {}
+
+        def finish_z(c):
+            crosstalk(nc.vector, n_pages - 1, chunks[c])
+            z_last[c] = ring.tile([P, CHUNK * PACK], BF16, name=f"z_last{c}", tag="h", bufs=6, align_bytes=64)
+            dst, src = weave_views(z_last[c][:], fac[last][:, :, chunks[c]])
+            if c in (0, 2):
+                nc.vector.tensor_scalar_max(dst, src, 0.0)
+            else:
+                nc.scalar.activation(dst, src, ACT.Relu)
+
+        def finish_product(c):
+            codes, scales = quantize(z_last[c][:], CHUNK, f"z_last_q{c}", "z_last_q", len(chunks))
+            product(last, c, codes, scales, slice(0, CHUNK))
+
+        def store(c):
+            result = ring.tile([P, N // P, CHUNK], F32, name=f"result{c}", tag="raw", bufs=3)
+            for pair in range(2):
+                dst = result[:, 2 * pair : 2 * pair + 2, :].rearrange("p n m -> p (n m)")
+                if pair == 0 and c >= 2:
+                    nc.vector.tensor_copy(dst, sums[c, pair][:])
                 else:
-                    nc.scalar.copy(result[:, n, :], sums[half, n][:])
-                nc.sync.dma_start(out[P * n : P * (n + 1), halves[half]], result[:, n, :])
+                    nc.scalar.copy(dst, sums[c, pair][:])
+            nc.sync.dma_start(out[:, chunks[c]].rearrange("(n p) m -> p n m", p=P), result[:])
+
+        finish_z(0)
+        finish_z(1)
+        finish_product(0)
+        finish_z(2)
+        finish_product(1)
+        finish_z(3)
+        store(0)
+        finish_product(2)
+        store(1)
+        finish_product(3)
+        store(2)
+        store(3)

@@ -22,13 +22,27 @@ PACK = 4
 PASS = P * PACK
 K_PASSES = K // PASS
 GROUPS = H // PASS
+LAST = GROUPS - 1
+PAGES = GROUPS * PACK
 QUADS = 4
 QUAD = P // QUADS
-BANK = 512
-BANKS = 8
+SCALE_ROWS = 4
 RUN = 4
 RUNS = P // RUN
+LINE = 4
+BANK = 512
+BANKS = 8
 CHUNK = 256
+CHUNKS = T2 // CHUNK
+
+RAW_BUFS = 3
+SMALL_BUFS = 6
+PAGE_BUFS = 6
+XT_BUFS = 2
+
+EARLY_PAGES = range(PACK, PACK + PAGE_BUFS)
+PAGE_PLACES = {0: "w1_bf00", 1: "w1_bf01", 2: "w1_bf10", 3: "w1_bf11", 10: "z_bf0", 11: "z_bf1"}
+W3_PLACES = ("tab2_s", "w2_s_raw", "tab_s")
 
 
 def tile_list_calorimeter_weave_kernel(
@@ -41,46 +55,50 @@ def tile_list_calorimeter_weave_kernel(
         ring = ctx.enter_context(tc.tile_pool(name="ring", bufs=1))
         psum = ctx.enter_context(tc.psum_pool(name="psum", bufs=1))
 
+
         def load_list(src, name):
             lst = keep.tile([P, S // 16], U16, name=name)
             nc.sync.dma_start(lst[:], src)
             return lst
 
         def load_words(src, a, name):
-            words = keep.tile([P, T], I32, name=name, align_bytes=64)
+            words = keep.tile([P, T], I32, name=name, tag=name, align_bytes=64)
             nc.sync.dma_start(words[:], src[a].rearrange("p t i -> p (t i)").bitcast(I32))
             return words
 
-        def gather(window, lst, dtype, name):
-            picked = keep.tile([P, S], dtype, name=name, align_bytes=64)
-            nc.vector.tensor_copy(picked[:], window.indirect(lst[:]))
-            return picked
+        def load_scales_by_column(tile, src):
+            for q in range(QUADS):
+                nc.sync.dma_start(
+                    tile[QUAD * q : QUAD * q + SCALE_ROWS].bitcast(I32),
+                    src[:, SCALE_ROWS * q : SCALE_ROWS * (q + 1), :].rearrange("a r c -> r a c").bitcast(I32),
+                )
 
         def load_gain(src, name):
-            raw = keep.tile([P, S], F32, name=name)
+            raw = ring.tile([P, S], F32, name=name, tag="page", bufs=PAGE_BUFS)
             nc.sync.dma_start(raw[:], src)
             return raw
 
-        def load_by_slot(tile, rows):
+        def load_w1(g):
+            raws = []
+            for a in range(K_PASSES):
+                raw = ring.tile([P, PACK, PASS], F32, name=f"w1_raw{g}{a}", tag="raw", bufs=RAW_BUFS)
+                rows = w1[PASS * a : PASS * (a + 1), PASS * g : PASS * (g + 1)]
+                nc.sync.dma_start(raw[:], rows.rearrange("(p i) c -> p i c", i=PACK))
+                raws.append(raw)
+            return raws
+
+        def load_in_page_order(tile, rows):
             for t in range(PACK):
                 nc.sync.dma_start(tile[:, t, :], rows.rearrange("(e t u) c -> t e u c", t=PACK, u=RUN)[t])
 
-        def load_rows(src, name):
-            raw = ring.tile([P, PACK, BANK], F32, name=name, tag="raw", bufs=3)
-            nc.sync.dma_start(raw[:], src.rearrange("(p i) c -> p i c", i=PACK))
-            return raw
-
         def load_xt(g):
-            fac = ring.tile([P, PACK, T2], F32, name=f"xt{g}", tag="xt", bufs=2)
-            load_by_slot(fac, xt[PASS * g : PASS * (g + 1), :])
-            return fac
+            factors = ring.tile([P, PACK, T2], F32, name=f"xt{g}", tag="xt", bufs=XT_BUFS)
+            load_in_page_order(factors, xt[PASS * g : PASS * (g + 1), :])
+            return factors
 
-        def bank(b, name):
-            return psum.tile([P, BANK], F32, name=name, tag=f"bank{b}")
-
-        tab2_s = keep.tile([P, K_PASSES, T], U8, name="tab2_s", align_bytes=64)
-        w2_s_raw = keep.tile([P, K_PASSES, H], U8, name="w2_s_raw", align_bytes=64)
-        tab_s = keep.tile([P, T], U8, name="tab_s", align_bytes=64)
+        tab2_s = keep.tile([P, K_PASSES, T], U8, name="tab2_s", tag="tab2_s", align_bytes=64)
+        w2_s_raw = keep.tile([P, K_PASSES, H], U8, name="w2_s_raw", tag="w2_s_raw", align_bytes=64)
+        tab_s = keep.tile([P, T], U8, name="tab_s", tag="tab_s", align_bytes=64)
         nc.gpsimd.memset(tab2_s[:].bitcast(I32), 0)
         nc.vector.memset(w2_s_raw[:].bitcast(I32), 0)
         nc.vector.memset(tab_s[:].bitcast(I32), 0)
@@ -88,38 +106,29 @@ def tile_list_calorimeter_weave_kernel(
         list2 = load_list(offs2, "list2")
         wg2_raw = load_gain(wg2, "wg2_raw")
         tab2_w = [load_words(tab2_words, 0, "tab2_w0")]
-        for q in range(QUADS):
-            nc.sync.dma_start(
-                tab2_s[QUAD * q : QUAD * q + 4].bitcast(I32),
-                tab2_scales[:, 4 * q : 4 * q + 4, :].rearrange("a r t -> r a t").bitcast(I32),
-            )
-        w2_w_raw = ring.tile([P, K_PASSES, H // 2], I32, name="w2_w_raw", tag="raw", bufs=3)
+        load_scales_by_column(tab2_s, tab2_scales)
+        w2_w_raw = ring.tile([P, K_PASSES, H // 2], I32, name="w2_w_raw", tag="raw", bufs=RAW_BUFS)
         nc.sync.dma_start(w2_w_raw[:], w2_words.rearrange("a p c -> p a c").bitcast(I32))
         tab2_w.append(load_words(tab2_words, 1, "tab2_w1"))
-        for q in range(QUADS):
-            nc.sync.dma_start(
-                w2_s_raw[QUAD * q : QUAD * q + 4].bitcast(I32),
-                w2_scales[:, 4 * q : 4 * q + 4, :].rearrange("a r c -> r a c").bitcast(I32),
-            )
-
+        load_scales_by_column(w2_s_raw, w2_scales)
         list4 = load_list(offs4, "list4")
-
-        def load_w1(g):
-            return [
-                load_rows(w1[PASS * a : PASS * (a + 1), PASS * g : PASS * (g + 1)], f"w1_raw{g}{a}")
-                for a in range(K_PASSES)
-            ]
 
         list1 = load_list(offs, "list1")
         for q in range(QUADS):
             nc.sync.dma_start(
-                tab_s[QUAD * q : QUAD * q + 4 * K_PASSES].bitcast(I32),
-                tab_scales[:, 4 * q : 4 * q + 4, :].bitcast(I32),
+                tab_s[QUAD * q : QUAD * q + SCALE_ROWS * K_PASSES].bitcast(I32),
+                tab_scales[:, SCALE_ROWS * q : SCALE_ROWS * (q + 1), :].bitcast(I32),
             )
         tab_w = [load_words(tab_words, a, f"tab_w{a}") for a in range(K_PASSES)]
         wg1_raw = load_gain(wg1, "wg1_raw")
         w1_raw = {0: load_w1(0)}
         list3 = load_list(offs3, "list3")
+
+
+        def gather(window, lst, dtype, name):
+            picked = keep.tile([P, S], dtype, name=name, align_bytes=64)
+            nc.vector.tensor_copy(picked[:], window.indirect(lst[:]))
+            return picked
 
         v2_w = [gather(tab2_w[0][:].bitcast(U32), list2, U32, "v2_w0")]
         v2_s = [gather(tab2_s[:, a, :], list2, U8, f"v2_s{a}") for a in range(K_PASSES)]
@@ -136,11 +145,15 @@ def tile_list_calorimeter_weave_kernel(
             w2_s_raw[:].bitcast(I32).rearrange("p a (g e t) -> p (a g) e t", t=PACK, e=RUNS),
         )
 
-        uses = [0]
+
+        def bank(b, name):
+            return psum.tile([P, BANK], F32, name=name, tag=f"bank{b}")
+
+        banks_taken = []
 
         def next_bank(name):
-            uses[0] = uses[0] + 1
-            return bank(uses[0] % BANKS, name)
+            banks_taken.append(name)
+            return bank(len(banks_taken) % BANKS, name)
 
         identity = keep.tile([P, P], F32, name="identity")
         make_identity(nc, identity[:])
@@ -151,7 +164,9 @@ def tile_list_calorimeter_weave_kernel(
                 nc.tensor.transpose(turned[:, P * c : P * (c + 1)], raw[:, P * c : P * (c + 1)], identity[:])
             spread = []
             for c in range(S // P):
-                piece = ring.tile([P, PACK * P], F32, name=f"{name}_spread{c}", tag="h", bufs=6, align_bytes=64)
+                piece = ring.tile(
+                    [P, PACK * P], F32, name=f"{name}_spread{c}", tag="small", bufs=SMALL_BUFS, align_bytes=64
+                )
                 rows = turned[:, P * c : P * (c + 1)].rearrange("j (e t u) -> j t e u", t=PACK, u=RUN)
                 nc.scalar.copy(
                     piece[:].rearrange("j (t q e u) -> j t q e u", t=PACK, q=QUADS, u=RUN),
@@ -166,14 +181,22 @@ def tile_list_calorimeter_weave_kernel(
                 nc.scalar.copy(gain[:, t, :], back[:])
             return gain
 
-        gain2 = order_gain(wg2_raw, "gain2")
+        responses, response_groups, pages, factors = {}, {}, {}, {}
+        w1_bf, w1_q, w3_bf, w3_q, z_bf, z_q = {}, {}, {}, {}, {}, {}
 
         def response_tile(stream, page):
-            h = ring.tile([P, S], F32, name=f"h{stream}_{page}", tag="h", bufs=6, align_bytes=64)
-            return h[:]
+            g, t = divmod(page, PACK)
+            if g == 0:
+                h = ring.tile([P, S], F32, name=f"h{stream}_{page}", tag="small", bufs=SMALL_BUFS, align_bytes=64)
+                return h[:]
+            if t == 0:
+                table = "tab2_w" if stream == 2 else "tab_w"
+                response_groups[stream, g] = keep.tile(
+                    [P, PACK, S], F32, name=f"h{stream}_{g}", tag=f"{table}{g - 1}", align_bytes=64
+                )
+            return response_groups[stream, g][:, t, :]
 
         def response2(page):
-            t = page % PACK
             acc = next_bank(f"b{page}")
             for a in range(K_PASSES):
                 cols = slice(H * a + P * page, H * a + P * (page + 1))
@@ -183,14 +206,14 @@ def tile_list_calorimeter_weave_kernel(
                     rhs=v2_w[a][:].bitcast(E4M3), rhs_scale=v2_s[a][:],
                     start=(a == 0), stop=(a == K_PASSES - 1),
                 )
-            h = response_tile(2, page)
-            nc.scalar.activation(h, acc[:], ACT.Abs)
-
-            resp[2, page] = h
+            responses[2, page] = response_tile(2, page)
+            nc.scalar.activation(responses[2, page], acc[:], ACT.Abs)
 
         def round_w1(g):
             for a in range(K_PASSES):
-                w1_bf[g, a] = ring.tile([P, PASS * PACK], BF16, name=f"w1_bf{g}{a}", tag=f"w1_bf{g}{a}", align_bytes=64)
+                w1_bf[g, a] = ring.tile(
+                    [P, PASS * PACK], BF16, name=f"w1_bf{g}{a}", tag=f"w1_bf{g}{a}", align_bytes=64
+                )
                 nc.scalar.copy(
                     w1_bf[g, a][:].rearrange("p (t e u i) -> p e t i u", t=PACK, u=RUN, i=PACK),
                     w1_raw[g][a][:].rearrange("p i (e t u) -> p e t i u", t=PACK, u=RUN),
@@ -204,7 +227,7 @@ def tile_list_calorimeter_weave_kernel(
 
         def quantize_w1(g):
             for a in range(K_PASSES):
-                w1_q[g, a] = quantize(w1_bf[g, a][:], PASS, f"w1_q{g}{a}", "w1_q", 2 * K_PASSES)
+                w1_q[g, a] = quantize(w1_bf[g, a][:], PASS, f"w1_q{g}{a}", "short_q", 2 * K_PASSES)
 
         def response1(page):
             g, t = divmod(page, PACK)
@@ -215,107 +238,122 @@ def tile_list_calorimeter_weave_kernel(
                 nc.tensor.matmul_mx(
                     out=acc[:],
                     lhsT=codes[:, cols].bitcast(E4M3), lhsT_scale=scales[:, cols],
-                    rhs=v_w[a][:].bitcast(E4M3), rhs_scale=v_s[4 * a : P, :],
+                    rhs=v_w[a][:].bitcast(E4M3), rhs_scale=v_s[SCALE_ROWS * a : P, :],
                     start=(a == 0), stop=(a == K_PASSES - 1),
                 )
             h = response_tile(1, page)
             nc.scalar.activation(h, acc[:], ACT.Square)
             nc.scalar.activation(h, h, ACT.Sqrt, bias=1.0)
-
-            resp[1, page] = h
+            responses[1, page] = h
 
         def scatter2(page):
-            if page in reuse:
-                pages[page] = ring.tile([P, T2], F32, name=f"page{page}", tag=reuse[page], align_bytes=64)
+            if page in PAGE_PLACES:
+                pages[page] = ring.tile([P, T2], F32, name=f"page{page}", tag=PAGE_PLACES[page], align_bytes=64)
             else:
-                pages[page] = ring.tile([P, T2], F32, name=f"page{page}", tag="page", bufs=4)
-            nc.vector.tensor_tensor(pages[page][:].indirect(list4[:]), resp[2, page], gain2[:, page % PACK, :], ALU.mult)
+                pages[page] = ring.tile([P, T2], F32, name=f"page{page}", tag="page", bufs=PAGE_BUFS)
+            window = pages[page][:].indirect(list4[:])
+            nc.vector.tensor_tensor(window, responses[2, page], gain2[:, page % PACK, :], ALU.mult)
 
         def scatter1(page):
-            nc.vector.tensor_tensor(pages[page][:].indirect(list3[:]), resp[1, page], gain1[:, page % PACK, :], ALU.mult)
+            window = pages[page][:].indirect(list3[:])
+            nc.vector.tensor_tensor(window, responses[1, page], gain1[:, page % PACK, :], ALU.mult)
 
-        def crosstalk(engine, page, cols):
+        def crosstalk(page, cols):
             g, t = divmod(page, PACK)
-            engine.tensor_tensor(fac[g][:, t, cols], pages[page][:, cols], fac[g][:, t, cols], ALU.mult)
+            nc.vector.tensor_tensor(factors[g][:, t, cols], pages[page][:, cols], factors[g][:, t, cols], ALU.mult)
+
+        def complete(page):
+            scatter1(page)
+            crosstalk(page, slice(0, T2))
+
 
         def weave_views(dst, src):
             return (
-                dst.rearrange("p (c i t) -> p c t i", t=PACK, i=4),
-                src.rearrange("p t (c i) -> p c t i", i=4),
+                dst.rearrange("p (c i t) -> p c t i", t=PACK, i=LINE),
+                src.rearrange("p t (c i) -> p c t i", i=LINE),
             )
 
         def round_w3(g):
-            raw = ring.tile([P, PACK, BANK], F32, name=f"w3_raw{g}", tag="raw", bufs=3)
-            load_by_slot(raw, w3[PASS * g : PASS * (g + 1), :])
-            w3_bf[g] = ring.tile([P, N * PACK], BF16, name=f"w3_bf{g}", tag="bf", bufs=2, align_bytes=64)
+            raw = ring.tile([P, PACK, N], F32, name=f"w3_raw{g}", tag="raw", bufs=RAW_BUFS)
+            load_in_page_order(raw, w3[PASS * g : PASS * (g + 1), :])
+            w3_bf[g] = keep.tile([P, N * PACK], BF16, name=f"w3_bf{g}", tag=W3_PLACES[g], align_bytes=64)
             nc.scalar.copy(*weave_views(w3_bf[g][:], raw[:]))
 
+        def quantize_w3(g):
+            w3_q[g] = quantize(w3_bf[g][:], N, f"w3_q{g}", "w3_q", GROUPS)
+
         def round_z(g):
-            z_bf[g] = ring.tile([P, T2 * PACK], BF16, name=f"z_bf{g}", tag="bf", bufs=2, align_bytes=64)
+            z_bf[g] = ring.tile([P, T2 * PACK], BF16, name=f"z_bf{g}", tag=f"z_bf{g}", align_bytes=64)
+            width = T2 // 2
             for half in range(2):
                 dst, src = weave_views(
-                    z_bf[g][:, BANK * PACK * half : BANK * PACK * (half + 1)], fac[g][:, :, halves[half]]
+                    z_bf[g][:, width * PACK * half : width * PACK * (half + 1)],
+                    factors[g][:, :, width * half : width * (half + 1)],
                 )
                 nc.scalar.activation(dst, src, ACT.Relu)
 
-        resp, pages, fac, w1_bf, w1_q, w3_bf, w3_q, z_bf, z_q = {}, {}, {}, {}, {}, {}, {}, {}, {}
-        halves = [slice(BANK * half, BANK * (half + 1)) for half in range(2)]
-        reuse = {3: "w1_bf00", 4: "w1_bf01", 7: "w1_bf10", 8: "w1_bf11", 10: "w1_bf20", 11: "w1_bf21"}
-        last = GROUPS - 1
-        n_pages = GROUPS * PACK
-        lead = 5
+        def quantize_z(g):
+            z_q[g] = quantize(z_bf[g][:], T2, f"z_q{g}", "z_q", LAST)
 
-        for page in range(3):
+
+        gain2 = order_gain(wg2_raw, "gain2")
+        for page in EARLY_PAGES:
             response2(page)
         gain1 = order_gain(wg1_raw, "gain1")
         round_w1(0)
-        fac[0] = load_xt(0)
         w1_raw[1] = load_w1(1)
-        for page in range(3):
+        round_w1(1)
+        w1_raw[2] = load_w1(2)
+        factors[0] = load_xt(0)
+        factors[1] = load_xt(1)
+        for page in EARLY_PAGES:
             scatter2(page)
         v_s = gather(tab_s[:], list1, U8, "v_s")
         v_w = [gather(tab_w[a][:].bitcast(U32), list1, U32, f"v_w{a}") for a in range(K_PASSES)]
+
         quantize_w1(0)
-        response2(3)
-        response2(4)
-        response1(0)
-        response2(5)
-        response1(1)
-        scatter2(3)
-        scatter2(4)
-        round_w1(1)
-        fac[1] = load_xt(1)
-        w1_raw[2] = load_w1(2)
+        for pair in ((0, 1), (2, 3)):
+            for page in pair:
+                response2(page)
+            for page in pair:
+                response1(page)
+        for page in (0, 1):
+            scatter2(page)
+        for page in (PAGES - 2, PAGES - 1):
+            response2(page)
+        for page in (0, 1):
+            complete(page)
+        quantize_w1(1)
+        round_w1(2)
+        for page in range(PACK, 2 * PACK):
+            response1(page)
+        for page in (2, 3):
+            scatter2(page)
+        for page in (2, 3):
+            complete(page)
+        quantize_w1(2)
+        for page in range(2 * PACK, PAGES):
+            response1(page)
+        for g in range(GROUPS):
+            round_w3(g)
+            quantize_w3(g)
+        round_z(0)
+        factors[2] = load_xt(2)
 
-        for page in range(n_pages - 1):
-            if page == 1:
-                quantize_w1(1)
-            if page == 2:
-                round_w1(2)
-            if page == 4:
-                quantize_w1(2)
-            if page + 2 < n_pages:
-                if page + 1 + lead < n_pages:
-                    response2(page + 1 + lead)
-                response1(page + 2)
-            scatter1(page)
-            if page + lead < n_pages:
-                scatter2(page + lead)
-            crosstalk(nc.vector, page, slice(0, T2))
-            if page % PACK == PACK - 1:
-                round_z(page // PACK)
-                if page // PACK + 2 < GROUPS:
-                    fac[page // PACK + 2] = load_xt(page // PACK + 2)
-            if page % PACK == 1 and page > PACK:
-                g = page // PACK - 1
-                z_q[g] = quantize(z_bf[g][:], T2, f"z_q{g}", "z_q", last)
-            if page in (5, 6, 7):
-                round_w3(page - 5)
-            if page in (6, 7, 8):
-                w3_q[page - 6] = quantize(w3_bf[page - 6][:], N, f"w3_q{page - 6}", "w3_q", GROUPS)
+        for page in range(PACK, 2 * PACK):
+            complete(page)
+        round_z(1)
+        for page in range(2 * PACK, PAGES - 2):
+            complete(page)
+        quantize_z(0)
+        scatter2(PAGES - 2)
+        complete(PAGES - 2)
+        quantize_z(1)
+        scatter2(PAGES - 1)
 
-        chunks = [slice(CHUNK * c, CHUNK * (c + 1)) for c in range(T2 // CHUNK)]
-        sums = {(c, pair): bank(2 * c + pair, f"sum{c}{pair}") for c in range(len(chunks)) for pair in range(2)}
+
+        chunks = [slice(CHUNK * c, CHUNK * (c + 1)) for c in range(CHUNKS)]
+        sums = {(c, pair): bank(2 * c + pair, f"sum{c}{pair}") for c in range(CHUNKS) for pair in range(2)}
 
         def product(g, c, z_codes, z_scales, cols):
             codes, scales = w3_q[g]
@@ -326,48 +364,48 @@ def tile_list_calorimeter_weave_kernel(
                     out=sums[c, pair][:, CHUNK * side : CHUNK * (side + 1)],
                     lhsT=codes[:, rows].bitcast(E4M3), lhsT_scale=scales[:, rows],
                     rhs=z_codes[:, cols].bitcast(E4M3), rhs_scale=z_scales[:, cols],
-                    start=(g == 0 and side == 0), stop=(g == last and side == 1),
+                    start=(g == 0 and side == 0), stop=(g == LAST and side == 1),
                 )
 
-        for g in range(last):
+        for g in range(LAST):
             for c, cols in enumerate(chunks):
                 product(g, c, *z_q[g], cols)
-        scatter1(n_pages - 1)
+        scatter1(PAGES - 1)
 
         z_last = {}
 
-        def finish_z(c):
-            crosstalk(nc.vector, n_pages - 1, chunks[c])
-            z_last[c] = ring.tile([P, CHUNK * PACK], BF16, name=f"z_last{c}", tag="h", bufs=6, align_bytes=64)
-            dst, src = weave_views(z_last[c][:], fac[last][:, :, chunks[c]])
-            if c in (0, 2):
+        def round_last_z(c):
+            crosstalk(PAGES - 1, chunks[c])
+            z_last[c] = ring.tile(
+                [P, CHUNK * PACK], BF16, name=f"z_last{c}", tag="small", bufs=SMALL_BUFS, align_bytes=64
+            )
+            dst, src = weave_views(z_last[c][:], factors[LAST][:, :, chunks[c]])
+            if c % 2 == 0:
                 nc.vector.tensor_scalar_max(dst, src, 0.0)
             else:
                 nc.scalar.activation(dst, src, ACT.Relu)
 
-        def finish_product(c):
-            codes, scales = quantize(z_last[c][:], CHUNK, f"z_last_q{c}", "z_last_q", len(chunks))
-            product(last, c, codes, scales, slice(0, CHUNK))
+        def last_product(c):
+            codes, scales = quantize(z_last[c][:], CHUNK, f"z_last_q{c}", "short_q", 2 * K_PASSES)
+            product(LAST, c, codes, scales, slice(0, CHUNK))
 
         def store(c):
-            result = ring.tile([P, N // P, CHUNK], F32, name=f"result{c}", tag="raw", bufs=3)
+            result = ring.tile([P, N // P, CHUNK], F32, name=f"result{c}", tag="page", bufs=PAGE_BUFS)
             for pair in range(2):
-                dst = result[:, 2 * pair : 2 * pair + 2, :].rearrange("p n m -> p (n m)")
-                if pair == 0 and c >= 2:
-                    nc.vector.tensor_copy(dst, sums[c, pair][:])
+                tiles = result[:, 2 * pair : 2 * pair + 2, :]
+                if pair == 0 and c >= CHUNKS // 2:
+                    nc.vector.tensor_copy(tiles.rearrange("p n m -> p (n m)"), sums[c, pair][:])
                 else:
-                    nc.scalar.copy(dst, sums[c, pair][:])
-            nc.sync.dma_start(out[:, chunks[c]].rearrange("(n p) m -> p n m", p=P), result[:])
+                    nc.scalar.copy(tiles.rearrange("p n m -> p (n m)"), sums[c, pair][:])
+                rows = out[2 * P * pair : 2 * P * (pair + 1), chunks[c]]
+                nc.sync.dma_start(rows.rearrange("(n p) m -> p n m", p=P), tiles)
 
-        finish_z(0)
-        finish_z(1)
-        finish_product(0)
-        finish_z(2)
-        finish_product(1)
-        finish_z(3)
-        store(0)
-        finish_product(2)
-        store(1)
-        finish_product(3)
-        store(2)
-        store(3)
+        for step in range(CHUNKS + 1):
+            if step < CHUNKS:
+                round_last_z(step)
+            if step >= 3:
+                store(step - 3)
+            if step >= 1:
+                last_product(step - 1)
+        for c in range(CHUNKS - 2, CHUNKS):
+            store(c)

from contextlib import ExitStack

import concourse.mybir as mybir
from concourse.masks import make_identity

K, T, S, T2, H, N = 1024, 2048, 512, 1024, 1536, 512
FLOPS = 2 * (2 * K * H * S + H * N * T2)

F32 = mybir.dt.float32
BF16 = mybir.dt.bfloat16
I32 = mybir.dt.int32
U32 = mybir.dt.uint32
U16 = mybir.dt.uint16
U8 = mybir.dt.uint8
E4M3 = mybir.dt.float8_e4m3fn_x4
E2M1 = mybir.dt.float4_e2m1fn_x4
ACT = mybir.ActivationFunctionType
ALU = mybir.AluOpType

P = 128
PACK = 4
PASS = P * PACK
K_PASSES = K // PASS
GROUPS = H // PASS
LAST = GROUPS - 1
PAGES = GROUPS * PACK
QUADS = 4
QUAD = P // QUADS
SCALE_ROWS = 4
RUN = 4
RUNS = P // RUN
LINE = 4
BANK = 512
BANKS = 8
CHUNK = 256
CHUNKS = T2 // CHUNK

RAW_BUFS = 3
SMALL_BUFS = 6
PAGE_BUFS = 6
XT_BUFS = 2

EARLY_PAGES = range(PACK, PACK + PAGE_BUFS)
PAGE_PLACES = {0: "w1_bf00", 1: "w1_bf01", 2: "w1_bf10", 3: "w1_bf11", 10: "z_bf0", 11: "z_bf1"}
W3_PLACES = ("tab2_s", "w2_s_raw", "tab_s")


def tile_list_calorimeter_weave_kernel(
    tc, tab_words, tab_scales, tab2_words, tab2_scales, offs, offs2, offs3, offs4,
    w1, w2_words, w2_scales, wg1, wg2, xt, w3, out,
):
    nc = tc.nc
    with ExitStack() as ctx:
        keep = ctx.enter_context(tc.tile_pool(name="keep", bufs=1))
        ring = ctx.enter_context(tc.tile_pool(name="ring", bufs=1))
        psum = ctx.enter_context(tc.psum_pool(name="psum", bufs=1))


        def load_list(src, name):
            lst = keep.tile([P, S // 16], U16, name=name)
            nc.sync.dma_start(lst[:], src)
            return lst

        def load_words(src, a, name):
            words = keep.tile([P, T], I32, name=name, tag=name, align_bytes=64)
            nc.sync.dma_start(words[:], src[a].rearrange("p t i -> p (t i)").bitcast(I32))
            return words

        def load_scales_by_column(tile, src):
            for q in range(QUADS):
                nc.sync.dma_start(
                    tile[QUAD * q : QUAD * q + SCALE_ROWS].bitcast(I32),
                    src[:, SCALE_ROWS * q : SCALE_ROWS * (q + 1), :].rearrange("a r c -> r a c").bitcast(I32),
                )

        def load_gain(src, name):
            raw = ring.tile([P, S], F32, name=name, tag="page", bufs=PAGE_BUFS)
            nc.sync.dma_start(raw[:], src)
            return raw

        def load_w1(g):
            raws = []
            for a in range(K_PASSES):
                raw = ring.tile([P, PACK, PASS], F32, name=f"w1_raw{g}{a}", tag="raw", bufs=RAW_BUFS)
                rows = w1[PASS * a : PASS * (a + 1), PASS * g : PASS * (g + 1)]
                nc.sync.dma_start(raw[:], rows.rearrange("(p i) c -> p i c", i=PACK))
                raws.append(raw)
            return raws

        def load_in_page_order(tile, rows):
            for t in range(PACK):
                nc.sync.dma_start(tile[:, t, :], rows.rearrange("(e t u) c -> t e u c", t=PACK, u=RUN)[t])

        def load_xt(g):
            factors = ring.tile([P, PACK, T2], F32, name=f"xt{g}", tag="xt", bufs=XT_BUFS)
            load_in_page_order(factors, xt[PASS * g : PASS * (g + 1), :])
            return factors

        tab2_s = keep.tile([P, K_PASSES, T], U8, name="tab2_s", tag="tab2_s", align_bytes=64)
        w2_s_raw = keep.tile([P, K_PASSES, H], U8, name="w2_s_raw", tag="w2_s_raw", align_bytes=64)
        tab_s = keep.tile([P, T], U8, name="tab_s", tag="tab_s", align_bytes=64)
        nc.gpsimd.memset(tab2_s[:].bitcast(I32), 0)
        nc.vector.memset(w2_s_raw[:].bitcast(I32), 0)
        nc.vector.memset(tab_s[:].bitcast(I32), 0)

        list2 = load_list(offs2, "list2")
        wg2_raw = load_gain(wg2, "wg2_raw")
        tab2_w = [load_words(tab2_words, 0, "tab2_w0")]
        load_scales_by_column(tab2_s, tab2_scales)
        w2_w_raw = ring.tile([P, K_PASSES, H // 2], I32, name="w2_w_raw", tag="raw", bufs=RAW_BUFS)
        nc.sync.dma_start(w2_w_raw[:], w2_words.rearrange("a p c -> p a c").bitcast(I32))
        tab2_w.append(load_words(tab2_words, 1, "tab2_w1"))
        load_scales_by_column(w2_s_raw, w2_scales)
        list4 = load_list(offs4, "list4")

        list1 = load_list(offs, "list1")
        for q in range(QUADS):
            nc.sync.dma_start(
                tab_s[QUAD * q : QUAD * q + SCALE_ROWS * K_PASSES].bitcast(I32),
                tab_scales[:, SCALE_ROWS * q : SCALE_ROWS * (q + 1), :].bitcast(I32),
            )
        tab_w = [load_words(tab_words, a, f"tab_w{a}") for a in range(K_PASSES)]
        wg1_raw = load_gain(wg1, "wg1_raw")
        w1_raw = {0: load_w1(0)}
        list3 = load_list(offs3, "list3")


        def gather(window, lst, dtype, name):
            picked = keep.tile([P, S], dtype, name=name, align_bytes=64)
            nc.vector.tensor_copy(picked[:], window.indirect(lst[:]))
            return picked

        v2_w = [gather(tab2_w[0][:].bitcast(U32), list2, U32, "v2_w0")]
        v2_s = [gather(tab2_s[:, a, :], list2, U8, f"v2_s{a}") for a in range(K_PASSES)]

        w2_w = keep.tile([P, K_PASSES * H // 2], I32, name="w2_w", align_bytes=64)
        w2_s = keep.tile([P, K_PASSES * H // 4], I32, name="w2_s", align_bytes=64)
        nc.vector.tensor_copy(
            w2_w[:].rearrange("p (b t e w) -> p b t e w", t=PACK, e=RUNS, w=2),
            w2_w_raw[:].rearrange("p a (g e t w) -> p (a g) t e w", t=PACK, e=RUNS, w=2),
        )
        v2_w.append(gather(tab2_w[1][:].bitcast(U32), list2, U32, "v2_w1"))
        nc.vector.tensor_copy(
            w2_s[:].rearrange("p (b t e) -> p b e t", t=PACK, e=RUNS),
            w2_s_raw[:].bitcast(I32).rearrange("p a (g e t) -> p (a g) e t", t=PACK, e=RUNS),
        )


        def bank(b, name):
            return psum.tile([P, BANK], F32, name=name, tag=f"bank{b}")

        banks_taken = []

        def next_bank(name):
            banks_taken.append(name)
            return bank(len(banks_taken) % BANKS, name)

        identity = keep.tile([P, P], F32, name="identity")
        make_identity(nc, identity[:])

        def order_gain(raw, name):
            turned = next_bank(name + "_turned")
            for c in range(S // P):
                nc.tensor.transpose(turned[:, P * c : P * (c + 1)], raw[:, P * c : P * (c + 1)], identity[:])
            spread = []
            for c in range(S // P):
                piece = ring.tile(
                    [P, PACK * P], F32, name=f"{name}_spread{c}", tag="small", bufs=SMALL_BUFS, align_bytes=64
                )
                rows = turned[:, P * c : P * (c + 1)].rearrange("j (e t u) -> j t e u", t=PACK, u=RUN)
                nc.scalar.copy(
                    piece[:].rearrange("j (t q e u) -> j t q e u", t=PACK, q=QUADS, u=RUN),
                    rows.unsqueeze(2).broadcast_to([P, PACK, QUADS, QUAD // RUN, RUN]),
                )
                spread.append(piece)
            gain = keep.tile([P, PACK, S], F32, name=name)
            for t in range(PACK):
                back = next_bank(f"{name}_back{t}")
                for c in range(S // P):
                    nc.tensor.transpose(back[:, P * c : P * (c + 1)], spread[c][:, P * t : P * (t + 1)], identity[:])
                nc.scalar.copy(gain[:, t, :], back[:])
            return gain

        responses, response_groups, pages, factors = {}, {}, {}, {}
        w1_bf, w1_q, w3_bf, w3_q, z_bf, z_q = {}, {}, {}, {}, {}, {}

        def response_tile(stream, page):
            g, t = divmod(page, PACK)
            if g == 0:
                h = ring.tile([P, S], F32, name=f"h{stream}_{page}", tag="small", bufs=SMALL_BUFS, align_bytes=64)
                return h[:]
            if t == 0:
                table = "tab2_w" if stream == 2 else "tab_w"
                response_groups[stream, g] = keep.tile(
                    [P, PACK, S], F32, name=f"h{stream}_{g}", tag=f"{table}{g - 1}", align_bytes=64
                )
            return response_groups[stream, g][:, t, :]

        def response2(page):
            acc = next_bank(f"b{page}")
            for a in range(K_PASSES):
                cols = slice(H * a + P * page, H * a + P * (page + 1))
                nc.tensor.matmul_mx(
                    out=acc[:],
                    lhsT=w2_w[:].bitcast(U16)[:, cols].bitcast(E2M1), lhsT_scale=w2_s[:].bitcast(U8)[:, cols],
                    rhs=v2_w[a][:].bitcast(E4M3), rhs_scale=v2_s[a][:],
                    start=(a == 0), stop=(a == K_PASSES - 1),
                )
            responses[2, page] = response_tile(2, page)
            nc.scalar.activation(responses[2, page], acc[:], ACT.Abs)

        def round_w1(g):
            for a in range(K_PASSES):
                w1_bf[g, a] = ring.tile(
                    [P, PASS * PACK], BF16, name=f"w1_bf{g}{a}", tag=f"w1_bf{g}{a}", align_bytes=64
                )
                nc.scalar.copy(
                    w1_bf[g, a][:].rearrange("p (t e u i) -> p e t i u", t=PACK, u=RUN, i=PACK),
                    w1_raw[g][a][:].rearrange("p i (e t u) -> p e t i u", t=PACK, u=RUN),
                )

        def quantize(rounded, width, name, tag, bufs):
            codes = ring.tile([P, width], U32, name=name + "_w", tag=tag + "_w", bufs=bufs, align_bytes=64)
            scales = ring.tile([P, width], U8, name=name + "_s", tag=tag + "_s", bufs=bufs, align_bytes=64)
            nc.vector.quantize_mx(out=codes[:].bitcast(E4M3), scales=scales[:], in_=rounded)
            return codes, scales

        def quantize_w1(g):
            for a in range(K_PASSES):
                w1_q[g, a] = quantize(w1_bf[g, a][:], PASS, f"w1_q{g}{a}", "short_q", 2 * K_PASSES)

        def response1(page):
            g, t = divmod(page, PACK)
            cols = slice(P * t, P * (t + 1))
            acc = next_bank(f"a{page}")
            for a in range(K_PASSES):
                codes, scales = w1_q[g, a]
                nc.tensor.matmul_mx(
                    out=acc[:],
                    lhsT=codes[:, cols].bitcast(E4M3), lhsT_scale=scales[:, cols],
                    rhs=v_w[a][:].bitcast(E4M3), rhs_scale=v_s[SCALE_ROWS * a : P, :],
                    start=(a == 0), stop=(a == K_PASSES - 1),
                )
            h = response_tile(1, page)
            nc.scalar.activation(h, acc[:], ACT.Square)
            nc.scalar.activation(h, h, ACT.Sqrt, bias=1.0)
            responses[1, page] = h

        def scatter2(page):
            if page in PAGE_PLACES:
                pages[page] = ring.tile([P, T2], F32, name=f"page{page}", tag=PAGE_PLACES[page], align_bytes=64)
            else:
                pages[page] = ring.tile([P, T2], F32, name=f"page{page}", tag="page", bufs=PAGE_BUFS)
            window = pages[page][:].indirect(list4[:])
            nc.vector.tensor_tensor(window, responses[2, page], gain2[:, page % PACK, :], ALU.mult)

        def scatter1(page):
            window = pages[page][:].indirect(list3[:])
            nc.vector.tensor_tensor(window, responses[1, page], gain1[:, page % PACK, :], ALU.mult)

        def crosstalk(page, cols):
            g, t = divmod(page, PACK)
            nc.vector.tensor_tensor(factors[g][:, t, cols], pages[page][:, cols], factors[g][:, t, cols], ALU.mult)

        def complete(page):
            scatter1(page)
            crosstalk(page, slice(0, T2))


        def weave_views(dst, src):
            return (
                dst.rearrange("p (c i t) -> p c t i", t=PACK, i=LINE),
                src.rearrange("p t (c i) -> p c t i", i=LINE),
            )

        def round_w3(g):
            raw = ring.tile([P, PACK, N], F32, name=f"w3_raw{g}", tag="raw", bufs=RAW_BUFS)
            load_in_page_order(raw, w3[PASS * g : PASS * (g + 1), :])
            w3_bf[g] = keep.tile([P, N * PACK], BF16, name=f"w3_bf{g}", tag=W3_PLACES[g], align_bytes=64)
            nc.scalar.copy(*weave_views(w3_bf[g][:], raw[:]))

        def quantize_w3(g):
            w3_q[g] = quantize(w3_bf[g][:], N, f"w3_q{g}", "w3_q", GROUPS)

        def round_z(g):
            z_bf[g] = ring.tile([P, T2 * PACK], BF16, name=f"z_bf{g}", tag=f"z_bf{g}", align_bytes=64)
            width = T2 // 2
            for half in range(2):
                dst, src = weave_views(
                    z_bf[g][:, width * PACK * half : width * PACK * (half + 1)],
                    factors[g][:, :, width * half : width * (half + 1)],
                )
                nc.scalar.activation(dst, src, ACT.Relu)

        def quantize_z(g):
            z_q[g] = quantize(z_bf[g][:], T2, f"z_q{g}", "z_q", LAST)


        gain2 = order_gain(wg2_raw, "gain2")
        for page in EARLY_PAGES:
            response2(page)
        gain1 = order_gain(wg1_raw, "gain1")
        round_w1(0)
        w1_raw[1] = load_w1(1)
        round_w1(1)
        w1_raw[2] = load_w1(2)
        factors[0] = load_xt(0)
        factors[1] = load_xt(1)
        for page in EARLY_PAGES:
            scatter2(page)
        v_s = gather(tab_s[:], list1, U8, "v_s")
        v_w = [gather(tab_w[a][:].bitcast(U32), list1, U32, f"v_w{a}") for a in range(K_PASSES)]

        quantize_w1(0)
        for pair in ((0, 1), (2, 3)):
            for page in pair:
                response2(page)
            for page in pair:
                response1(page)
        for page in (0, 1):
            scatter2(page)
        for page in (PAGES - 2, PAGES - 1):
            response2(page)
        for page in (0, 1):
            complete(page)
        quantize_w1(1)
        round_w1(2)
        for page in range(PACK, 2 * PACK):
            response1(page)
        for page in (2, 3):
            scatter2(page)
        for page in (2, 3):
            complete(page)
        quantize_w1(2)
        for page in range(2 * PACK, PAGES):
            response1(page)
        for g in range(GROUPS):
            round_w3(g)
            quantize_w3(g)
        round_z(0)
        factors[2] = load_xt(2)

        for page in range(PACK, 2 * PACK):
            complete(page)
        round_z(1)
        for page in range(2 * PACK, PAGES - 2):
            complete(page)
        quantize_z(0)
        scatter2(PAGES - 2)
        complete(PAGES - 2)
        quantize_z(1)
        scatter2(PAGES - 1)


        chunks = [slice(CHUNK * c, CHUNK * (c + 1)) for c in range(CHUNKS)]
        sums = {(c, pair): bank(2 * c + pair, f"sum{c}{pair}") for c in range(CHUNKS) for pair in range(2)}

        def product(g, c, z_codes, z_scales, cols):
            codes, scales = w3_q[g]
            for n in range(N // P):
                rows = slice(P * n, P * (n + 1))
                pair, side = divmod(n, 2)
                nc.tensor.matmul_mx(
                    out=sums[c, pair][:, CHUNK * side : CHUNK * (side + 1)],
                    lhsT=codes[:, rows].bitcast(E4M3), lhsT_scale=scales[:, rows],
                    rhs=z_codes[:, cols].bitcast(E4M3), rhs_scale=z_scales[:, cols],
                    start=(g == 0 and side == 0), stop=(g == LAST and side == 1),
                )

        for g in range(LAST):
            for c, cols in enumerate(chunks):
                product(g, c, *z_q[g], cols)
        scatter1(PAGES - 1)

        z_last = {}

        def round_last_z(c):
            crosstalk(PAGES - 1, chunks[c])
            z_last[c] = ring.tile(
                [P, CHUNK * PACK], BF16, name=f"z_last{c}", tag="small", bufs=SMALL_BUFS, align_bytes=64
            )
            dst, src = weave_views(z_last[c][:], factors[LAST][:, :, chunks[c]])
            if c % 2 == 0:
                nc.vector.tensor_scalar_max(dst, src, 0.0)
            else:
                nc.scalar.activation(dst, src, ACT.Relu)

        def last_product(c):
            codes, scales = quantize(z_last[c][:], CHUNK, f"z_last_q{c}", "short_q", 2 * K_PASSES)
            product(LAST, c, codes, scales, slice(0, CHUNK))

        def store(c):
            result = ring.tile([P, N // P, CHUNK], F32, name=f"result{c}", tag="page", bufs=PAGE_BUFS)
            for pair in range(2):
                tiles = result[:, 2 * pair : 2 * pair + 2, :]
                if pair == 0 and c >= CHUNKS // 2:
                    nc.vector.tensor_copy(tiles.rearrange("p n m -> p (n m)"), sums[c, pair][:])
                else:
                    nc.scalar.copy(tiles.rearrange("p n m -> p (n m)"), sums[c, pair][:])
                rows = out[2 * P * pair : 2 * P * (pair + 1), chunks[c]]
                nc.sync.dma_start(rows.rearrange("(n p) m -> p n m", p=P), tiles)

        for step in range(CHUNKS + 1):
            if step < CHUNKS:
                round_last_z(step)
            if step >= 3:
                store(step - 3)
            if step >= 1:
                last_product(step - 1)
        for c in range(CHUNKS - 2, CHUNKS):
            store(c)
